import numpy as np
import ml_dtypes


def mxq(x, axis, fmt="e4m3"):
    dtype, down = {"e4m3": (ml_dtypes.float8_e4m3fn, 7), "e5m2": (ml_dtypes.float8_e5m2, 14)}[fmt]
    v = np.moveaxis(np.asarray(x, np.float32).astype(ml_dtypes.bfloat16).astype(np.float64), axis, -1)
    blocks = v.reshape(v.shape[:-1] + (-1, 32))
    amax = np.abs(blocks).max(-1, keepdims=True)
    byte = np.maximum(np.where(amax > 0, np.frexp(amax)[1] - 1 + 127, 0) - down, 1)
    scale = np.exp2(byte - 127.0)
    codes = (blocks / scale).astype(np.float32).astype(dtype).astype(np.float64)
    return np.moveaxis((codes * scale).reshape(v.shape), -1, axis)


WIDE = False


def mx_kscale(k):
    if not WIDE:
        return np.ones(k)
    levels = np.array([10, -10, 5, -5, 0])
    if k % 512:
        return np.exp2(np.random.permutation(np.resize(levels, k // 32))).repeat(32)
    a = np.empty((k // 512, 16))
    for p in range(k // 512):
        a[p, :8] = np.random.permutation(np.resize(levels, 8))
        for g in range(8):
            far = levels[np.abs(levels - a[p, g]) >= 10]
            a[p, g + 8] = far[np.random.randint(len(far))]
    return np.exp2(a.ravel()).repeat(32)


def f64(x):
    return np.asarray(x).astype(np.float64)


def striped(idx):
    return np.tile(idx.reshape(-1, 16).T, (8, 1)).astype(np.uint16)


def unstriped(offs):
    return offs[:16].T.reshape(-1).astype(np.int64)


def striped8(idx):
    return np.concatenate([x.reshape(-1, 16).T for x in idx]).astype(np.uint16)


def runs(offs, k):
    lists = np.stack([offs[16 * r : 16 * r + 16].T.reshape(-1) for r in range(8)]).astype(np.int64)
    return lists[np.arange(k) % 512 // 64]


def pack_weight(w):
    k, n = w.shape
    w = f64(np.asarray(w, np.float32).astype(ml_dtypes.bfloat16)).reshape(k // 32, 32, n)
    amax = np.abs(w).max(1)
    byte = np.clip(np.where(amax > 0, np.frexp(amax)[1] - 1 + 127 - 7, 1), 1, 254)
    scaled = (w * np.exp2(127.0 - byte)[:, None, :]).reshape(k, n).astype(np.float32)
    words = np.ascontiguousarray(scaled.reshape(k // 512, 128, 4, n).transpose(0, 1, 3, 2)).astype(ml_dtypes.float8_e4m3fn).view(np.uint8)
    return words, np.ascontiguousarray(byte.astype(np.uint8).reshape(k // 512, 16, n))


def unpack_weight(words, scales):
    g, p, n, _ = words.shape
    vals = np.ascontiguousarray(words).view(ml_dtypes.float8_e4m3fn).astype(np.float64) * np.repeat(np.exp2(scales.astype(np.float64) - 127.0), 8, axis=1)[..., None]
    return vals.transpose(0, 1, 3, 2).reshape(g * 512, n)


def sigmoid(v):
    return 1.0 / (1.0 + np.exp(-np.maximum(v, -700.0)))


K, T, S, G, H, C = 512, 1024, 512, 2048, 512, 512


def setup_inputs():
    n = np.random.standard_normal
    s = mx_kscale(K)[:, None]
    packed_xT = pack_weight(n((K, T)) * s)
    packed_dT = pack_weight(n((K, G)) / s)
    return {
        "x_words": packed_xT[0],
        "x_scales": packed_xT[1],
        "d_words": packed_dT[0],
        "d_scales": packed_dT[1],
        "gs": (np.random.uniform(0.5, 1.5, (K, 1)) / s).astype(np.float32),
        "offs": striped(np.random.permutation(T)[:S]),
        "k1": striped8(np.random.randint(0, G, (8, H))),
        "n1": striped(np.random.permutation(S)),
        "n2": striped(np.random.permutation(S)),
        "cand": striped(np.random.permutation(T)[:C]),
        "two": striped(np.random.permutation(T)[:S]),
        "k2": striped8(np.random.randint(0, G, (8, H))),
        "n3": striped8(np.stack([np.random.permutation(S) for _ in range(8)])),
        "n4": striped8(np.stack([np.random.permutation(S) for _ in range(8)])),
    }


def reference(x_words, x_scales, d_words, d_scales, gs, offs, k1, n1, n2, cand, two, k2, n3, n4):
    x_cand = unpack_weight(x_words, x_scales)[:, unstriped(cand)]
    d_k1 = unpack_weight(d_words, d_scales)[np.arange(K)[:, None], runs(k1, K)]
    xq = unpack_weight(x_words, x_scales)[:, unstriped(offs)]
    h = 0.0625 * (d_k1.T @ xq)
    sm = np.maximum(h, h[:, unstriped(n2)])
    ds = np.zeros((H, S))
    ds[:, unstriped(n1)] = sm
    z = f64(gs) * (ds * sigmoid(h))
    a = 0.0625 * ((x_cand.T @ mxq(z, 0, "e4m3")))
    d_k2 = unpack_weight(d_words, d_scales)[np.arange(K)[:, None], runs(k2, K)]
    x_two = unpack_weight(x_words, x_scales)[:, unstriped(two)]
    b = 0.0625 * (d_k2.T @ x_two)
    return a[np.arange(C)[:, None], runs(n3, C)] - (np.tanh(b) * (b[np.arange(H)[:, None], runs(n4, H)]))

@@ -1,0 +1,207 @@
+from contextlib import ExitStack
+
+import concourse.mybir as mybir
+
+K, T, S, G, H, C = 512, 1024, 512, 2048, 512, 512
+FLOPS = 3 * 2 * 512 * 512 * 512
+
+F32 = mybir.dt.float32
+BF16 = mybir.dt.bfloat16
+U32 = mybir.dt.uint32
+I32 = mybir.dt.int32
+U16 = mybir.dt.uint16
+U8 = mybir.dt.uint8
+FP8X4 = mybir.dt.float8_e4m3fn_x4
+ACT = mybir.ActivationFunctionType
+ALU = mybir.AluOpType
+
+P = 128
+PACK = 4
+HALF = S // 2
+SIXTEENTH = 0.0625
+H_SPARE = 16
+DS_WIDE = 704
+
+
+def tile_picked_pqcjsoftbsendg_none_p_kernel(
+    tc, x_words, x_scales, d_words, d_scales, gs, offs, k1, n1, n2, cand, two, k2, n3, n4, out
+):
+    nc = tc.nc
+    with ExitStack() as ctx:
+        lists = ctx.enter_context(tc.tile_pool(name="lists", bufs=1))
+        keep = ctx.enter_context(tc.tile_pool(name="keep", bufs=1))
+        psum = ctx.enter_context(tc.psum_pool(name="psum", bufs=1))
+
+        def load_list(name, dram):
+            tile = lists.tile([P, S // 16], U16, name=name)
+            nc.sync.dma_start(tile[:], dram)
+            return tile
+
+        def half(offsets, u):
+            return offsets[:, 16 * u : 16 * (u + 1)]
+
+        def cols(u):
+            return slice(HALF * u, HALF * (u + 1))
+
+        d_scale_win = keep.tile([P, G], U8, name="d_scale_win", align_bytes=64)
+        x_scale_win = keep.tile([P, T], U8, name="x_scale_win", align_bytes=64)
+        nc.gpsimd.memset(d_scale_win[:].bitcast(I32), 0)
+        nc.vector.memset(x_scale_win[:].bitcast(I32), 0)
+        k1_list = load_list("k1_list", k1)
+        nc.sync.dma_start(d_scale_win[0:P:8, :].bitcast(I32), d_scales[0].bitcast(I32))
+        offs_list = load_list("offs_list", offs)
+        for r in range(PACK):
+            nc.sync.dma_start(x_scale_win[r:P:32, :].bitcast(I32), x_scales[0, r:16:PACK, :].bitcast(I32))
+        x_win = keep.tile([P, T], I32, name="x_win", align_bytes=64)
+        d_win = keep.tile([P, G], I32, name="d_win", align_bytes=64)
+        nc.sync.dma_start(x_win[:], x_words[0].rearrange("p n t -> p (n t)").bitcast(I32))
+        nc.sync.dma_start(d_win[:], d_words[0].rearrange("p n t -> p (n t)").bitcast(I32))
+        gs_tile = keep.tile([P, PACK], F32, name="gs_tile")
+
+
+        def coded_scales(name, offsets):
+            plane = keep.tile([P, H], U8, name=name + "_plane", align_bytes=64)
+            nc.gpsimd.memset(plane[:].bitcast(I32), 0)
+            picked = keep.tile([P, H], U8, name=name + "_picked_scales", align_bytes=64)
+            nc.vector.tensor_copy(picked[:], d_scale_win[:].indirect(offsets[:]))
+            dealt = keep.tile([P, H], U8, name=name + "_dealt_scales", align_bytes=64)
+            nc.vector.tensor_copy(
+                dealt[:].rearrange("p (t m) -> p m t", t=PACK), picked[:].rearrange("p (m t) -> p m t", t=PACK)
+            )
+            for r in range(PACK):
+                nc.sync.dma_start(plane[r:P:32, :].bitcast(I32), dealt[8 * r : P : 32, :].bitcast(I32))
+            return plane
+
+        def coded_words(name, offsets):
+            picked = keep.tile([P, H], U32, name=name + "_picked_words", align_bytes=64)
+            nc.vector.tensor_copy(picked[:], d_win[:].bitcast(U32).indirect(offsets[:]))
+            dealt = keep.tile([P, H], U32, name=name + "_dealt_words", align_bytes=64)
+            nc.vector.tensor_copy(
+                dealt[:].rearrange("p (t m) -> p m t", t=PACK), picked[:].rearrange("p (m t) -> p m t", t=PACK)
+            )
+            return dealt
+
+        def token_scales(name, offsets, deal):
+            picked = keep.tile([P, S], U8, name=name + "_scales", align_bytes=64)
+            view = picked[:].rearrange("p (t m) -> p m t", t=PACK) if deal else picked[:]
+            nc.vector.tensor_copy(view, x_scale_win[:].indirect(offsets[:]))
+            return picked
+
+        def token_words(name, offsets, deal):
+            picked = keep.tile([P, S], U32, name=name + "_words", align_bytes=64)
+            view = picked[:].rearrange("p (t m) -> p m t", t=PACK) if deal else picked[:]
+            nc.vector.tensor_copy(view, x_win[:].bitcast(U32).indirect(offsets[:]))
+            return picked
+
+        def products(tag, lhs_words, lhs_scales, rhs_words, rhs_scales):
+            banks = []
+            for t in range(PACK):
+                bank = psum.tile([P, S], F32, name=tag + str(t))
+                m = slice(P * t, P * (t + 1))
+                nc.tensor.matmul_mx(
+                    out=bank[:],
+                    lhsT=lhs_words[:, m].bitcast(FP8X4),
+                    lhsT_scale=lhs_scales[:, m],
+                    rhs=rhs_words[:].bitcast(FP8X4),
+                    rhs_scale=rhs_scales[:],
+                    start=True,
+                    stop=True,
+                )
+                banks.append(bank)
+            return banks
+
+        k1_scales = coded_scales("k1", k1_list)
+        offs_scales = token_scales("offs", offs_list, False)
+        offs_words = token_words("offs", offs_list, False)
+        k1_words = coded_words("k1", k1_list)
+        h_banks = products("first", k1_words, k1_scales, offs_words, offs_scales)
+
+        k2_list = load_list("k2_list", k2)
+        two_list = load_list("two_list", two)
+        n2_list = load_list("n2_list", n2)
+        cand_list = load_list("cand_list", cand)
+        n1_list = load_list("n1_list", n1)
+        n4_list = load_list("n4_list", n4)
+        n3_list = load_list("n3_list", n3)
+        nc.sync.dma_start(gs_tile[:], gs.rearrange("(p t) o -> p (t o)", t=PACK))
+
+        h = [keep.tile([P, S + H_SPARE], F32, name="h%d" % t) for t in range(PACK)]
+        h_n2 = [keep.tile([P, S], F32, name="h_n2_%d" % t) for t in range(PACK)]
+        sig = [keep.tile([P, S], F32, name="sig%d" % t) for t in range(PACK)]
+        sm = [keep.tile([P, S], F32, name="sm%d" % t) for t in range(PACK)]
+        ds = [keep.tile([P, S if t < 2 else DS_WIDE], F32, name="ds%d" % t) for t in range(PACK)]
+        b = [keep.tile([P, S], F32, name="b%d" % t) for t in range(PACK)]
+        tanh_b = [keep.tile([P, S], F32, name="tanh_b%d" % t) for t in range(PACK)]
+        tb = [keep.tile([P, S], F32, name="tb%d" % t) for t in range(PACK)]
+        a = [keep.tile([P, S], F32, name="a%d" % t) for t in range(PACK)]
+        res = [keep.tile([P, S], F32, name="res%d" % t) for t in range(PACK)]
+        for t in range(PACK):
+            nc.gpsimd.memset(h[t][:, S:], 0.0)
+
+        def sigmoid(t):
+            nc.scalar.activation(sig[t][:], h_banks[t][:], ACT.Sigmoid, scale=SIXTEENTH)
+
+        sigmoid(0)
+        for t in range(PACK):
+            nc.scalar.activation(h[t][:, :S], h_banks[t][:], ACT.Copy, scale=SIXTEENTH)
+            nc.scalar.activation(h_n2[t][:], h[t][:].indirect(n2_list[:]), ACT.Copy)
+
+        def larger(t):
+            nc.vector.tensor_tensor(sm[t][:], h[t][:, :S], h_n2[t][:], ALU.max)
+
+        k2_scales = coded_scales("k2", k2_list)
+        k2_words = coded_words("k2", k2_list)
+        two_scales = token_scales("two", two_list, False)
+        two_words = token_words("two", two_list, False)
+        b_banks = products("second", k2_words, k2_scales, two_words, two_scales)
+        larger(0)
+        larger(1)
+        cand_scales = token_scales("cand", cand_list, True)
+        cand_words = token_words("cand", cand_list, True)
+        larger(2)
+        larger(3)
+
+        for u in range(2):
+            for t in range(2):
+                nc.scalar.activation(ds[t][:].indirect(half(n1_list, u)), sm[t][:, cols(u)], ACT.Copy)
+            if u == 0:
+                for t in range(1, PACK):
+                    sigmoid(t)
+        for t in range(2, PACK):
+            nc.vector.tensor_copy(ds[t][:].indirect(n1_list[:]), sm[t][:])
+
+        z_rows = keep.tile([P, PACK, S], BF16, name="z_rows", align_bytes=64)
+        for t in (2, 3, 0, 1):
+            nc.vector.scalar_tensor_tensor(
+                z_rows[:, t, :], ds[t][:, :S], gs_tile[:, t : t + 1], sig[t][:], ALU.mult, ALU.mult
+            )
+        z_woven = keep.tile([P, S, PACK], BF16, name="z_woven", align_bytes=64)
+        nc.vector.tensor_copy(
+            z_woven[:].rearrange("p (c i) t -> p c t i", i=4), z_rows[:].rearrange("p t (c i) -> p c t i", i=4)
+        )
+        z_words = keep.tile([P, S], U32, name="z_words", align_bytes=64)
+        z_scales = keep.tile([P, S], U8, name="z_scales", align_bytes=64)
+        nc.vector.quantize_mx(
+            out=z_words[:].bitcast(FP8X4), scales=z_scales[:], in_=z_woven[:].rearrange("p c t -> p (c t)")
+        )
+
+        for t in range(PACK):
+            nc.scalar.activation(b[t][:], b_banks[t][:], ACT.Copy, scale=SIXTEENTH)
+            nc.scalar.activation(tanh_b[t][:], b_banks[t][:], ACT.Tanh, scale=SIXTEENTH)
+
+        a_banks = products("first", cand_words, cand_scales, z_words, z_scales)
+        for t in range(PACK):
+            nc.scalar.activation(a[t][:], a_banks[t][:], ACT.Copy, scale=SIXTEENTH)
+
+        out_rows = out.rearrange("(p t) c -> t p c", t=PACK)
+        for t in range(PACK):
+            for u in range(2):
+                nc.vector.tensor_tensor(
+                    tb[t][:, cols(u)], b[t][:].indirect(half(n4_list, u)), tanh_b[t][:, cols(u)], ALU.mult
+                )
+        for t in range(PACK):
+            for u in range(2):
+                nc.vector.tensor_tensor(
+                    res[t][:, cols(u)], a[t][:].indirect(half(n3_list, u)), tb[t][:, cols(u)], ALU.subtract
+                )
+            nc.sync.dma_start(out_rows[t], res[t][:])

@@ -19,7 +19,7 @@ P = 128
 PACK = 4
 HALF = S // 2
 SIXTEENTH = 0.0625
-H_SPARE = 16
+H_STRETCHES = ((0, 128), (128, 128), (256, 256))
 DS_WIDE = 704
 
 
@@ -45,24 +45,23 @@ def tile_picked_pqcjsoftbsendg_none_p_kernel(
 
         d_scale_win = keep.tile([P, G], U8, name="d_scale_win", align_bytes=64)
         x_scale_win = keep.tile([P, T], U8, name="x_scale_win", align_bytes=64)
-        nc.gpsimd.memset(d_scale_win[:].bitcast(I32), 0)
-        nc.vector.memset(x_scale_win[:].bitcast(I32), 0)
+        nc.vector.memset(d_scale_win[:].bitcast(I32), 0)
+        nc.gpsimd.memset(x_scale_win[:].bitcast(I32), 0)
         k1_list = load_list("k1_list", k1)
         nc.sync.dma_start(d_scale_win[0:P:8, :].bitcast(I32), d_scales[0].bitcast(I32))
         offs_list = load_list("offs_list", offs)
-        for r in range(PACK):
-            nc.sync.dma_start(x_scale_win[r:P:32, :].bitcast(I32), x_scales[0, r:16:PACK, :].bitcast(I32))
         x_win = keep.tile([P, T], I32, name="x_win", align_bytes=64)
         d_win = keep.tile([P, G], I32, name="d_win", align_bytes=64)
-        nc.sync.dma_start(x_win[:], x_words[0].rearrange("p n t -> p (n t)").bitcast(I32))
+        for r in range(PACK):
+            nc.sync.dma_start(x_scale_win[r:P:32, :].bitcast(I32), x_scales[0, r:16:PACK, :].bitcast(I32))
         nc.sync.dma_start(d_win[:], d_words[0].rearrange("p n t -> p (n t)").bitcast(I32))
+        nc.sync.dma_start(x_win[:], x_words[0].rearrange("p n t -> p (n t)").bitcast(I32))
         gs_tile = keep.tile([P, PACK], F32, name="gs_tile")
 
-
-        def coded_scales(name, offsets):
+        def coded_scales(name, offsets, tag):
             plane = keep.tile([P, H], U8, name=name + "_plane", align_bytes=64)
-            nc.gpsimd.memset(plane[:].bitcast(I32), 0)
-            picked = keep.tile([P, H], U8, name=name + "_picked_scales", align_bytes=64)
+            nc.vector.memset(plane[:].bitcast(I32), 0)
+            picked = keep.tile([P, H], U8, name=name + "_picked_scales", tag=tag, align_bytes=64)
             nc.vector.tensor_copy(picked[:], d_scale_win[:].indirect(offsets[:]))
             dealt = keep.tile([P, H], U8, name=name + "_dealt_scales", align_bytes=64)
             nc.vector.tensor_copy(
@@ -72,8 +71,8 @@ def tile_picked_pqcjsoftbsendg_none_p_kernel(
                 nc.sync.dma_start(plane[r:P:32, :].bitcast(I32), dealt[8 * r : P : 32, :].bitcast(I32))
             return plane
 
-        def coded_words(name, offsets):
-            picked = keep.tile([P, H], U32, name=name + "_picked_words", align_bytes=64)
+        def coded_words(name, offsets, tag):
+            picked = keep.tile([P, H], U32, name=name + "_picked_words", tag=tag, align_bytes=64)
             nc.vector.tensor_copy(picked[:], d_win[:].bitcast(U32).indirect(offsets[:]))
             dealt = keep.tile([P, H], U32, name=name + "_dealt_words", align_bytes=64)
             nc.vector.tensor_copy(
@@ -81,14 +80,14 @@ def tile_picked_pqcjsoftbsendg_none_p_kernel(
             )
             return dealt
 
-        def token_scales(name, offsets, deal):
-            picked = keep.tile([P, S], U8, name=name + "_scales", align_bytes=64)
+        def token_scales(name, offsets, deal, tag):
+            picked = keep.tile([P, S], U8, name=name + "_scales", tag=tag, align_bytes=64)
             view = picked[:].rearrange("p (t m) -> p m t", t=PACK) if deal else picked[:]
             nc.vector.tensor_copy(view, x_scale_win[:].indirect(offsets[:]))
             return picked
 
-        def token_words(name, offsets, deal):
-            picked = keep.tile([P, S], U32, name=name + "_words", align_bytes=64)
+        def token_words(name, offsets, deal, tag):
+            picked = keep.tile([P, S], U32, name=name + "_words", tag=tag, align_bytes=64)
             view = picked[:].rearrange("p (t m) -> p m t", t=PACK) if deal else picked[:]
             nc.vector.tensor_copy(view, x_win[:].bitcast(U32).indirect(offsets[:]))
             return picked
@@ -110,11 +109,36 @@ def tile_picked_pqcjsoftbsendg_none_p_kernel(
                 banks.append(bank)
             return banks
 
-        k1_scales = coded_scales("k1", k1_list)
-        offs_scales = token_scales("offs", offs_list, False)
-        offs_words = token_words("offs", offs_list, False)
-        k1_words = coded_words("k1", k1_list)
-        h_banks = products("first", k1_words, k1_scales, offs_words, offs_scales)
+        k1_scales = coded_scales("k1", k1_list, "k1_scales")
+        lead = H_STRETCHES[0][1]
+        lead_scales = keep.tile([P, lead], U8, name="lead_scales", tag="scales_in_turn", align_bytes=64)
+        rest_scales = keep.tile([P, S - lead], U8, name="rest_scales", align_bytes=64)
+        nc.vector.tensor_copy(lead_scales[:], x_scale_win[:].indirect(offs_list[:, : lead // 16]))
+        nc.vector.tensor_copy(rest_scales[:], x_scale_win[:].indirect(offs_list[:, lead // 16 :]))
+        k1_words = coded_words("k1", k1_list, "k1_words")
+        h_parts = []
+        for first, width in H_STRETCHES:
+            stretch = slice(first, first + width)
+            entries = offs_list[:, first // 16 : (first + width) // 16]
+            offs_scales = lead_scales[:] if first == 0 else rest_scales[:, first - lead : first - lead + width]
+            words_tag = "words_in_turn" if first == 0 else "offs_words%d" % first
+            offs_words = keep.tile([P, width], U32, name="offs_words", tag=words_tag, align_bytes=64)
+            nc.vector.tensor_copy(offs_words[:], x_win[:].bitcast(U32).indirect(entries))
+            per_bank = S // width
+            for t0 in range(0, PACK, per_bank):
+                bank = psum.tile([P, per_bank, width], F32, name="first%d" % len(h_parts))
+                for t in range(t0, t0 + per_bank):
+                    m = slice(P * t, P * (t + 1))
+                    nc.tensor.matmul_mx(
+                        out=bank[:, t - t0, :],
+                        lhsT=k1_words[:, m].bitcast(FP8X4),
+                        lhsT_scale=k1_scales[:, m],
+                        rhs=offs_words[:].bitcast(FP8X4),
+                        rhs_scale=offs_scales,
+                        start=True,
+                        stop=True,
+                    )
+                h_parts.append((bank, slice(t0, t0 + per_bank), stretch))
 
         k2_list = load_list("k2_list", k2)
         two_list = load_list("two_list", two)
@@ -125,56 +149,58 @@ def tile_picked_pqcjsoftbsendg_none_p_kernel(
         n3_list = load_list("n3_list", n3)
         nc.sync.dma_start(gs_tile[:], gs.rearrange("(p t) o -> p (t o)", t=PACK))
 
-        h = [keep.tile([P, S + H_SPARE], F32, name="h%d" % t) for t in range(PACK)]
+        h = keep.tile([P, PACK, S], F32, name="h", align_bytes=64)
         h_n2 = [keep.tile([P, S], F32, name="h_n2_%d" % t) for t in range(PACK)]
-        sig = [keep.tile([P, S], F32, name="sig%d" % t) for t in range(PACK)]
-        sm = [keep.tile([P, S], F32, name="sm%d" % t) for t in range(PACK)]
+        sig = keep.tile([P, PACK, S], F32, name="sig")
+        sm = [keep.tile([P, S], F32, name="sm%d" % t, align_bytes=64) for t in range(PACK)]
         ds = [keep.tile([P, S if t < 2 else DS_WIDE], F32, name="ds%d" % t) for t in range(PACK)]
         b = [keep.tile([P, S], F32, name="b%d" % t) for t in range(PACK)]
         tanh_b = [keep.tile([P, S], F32, name="tanh_b%d" % t) for t in range(PACK)]
         tb = [keep.tile([P, S], F32, name="tb%d" % t) for t in range(PACK)]
         a = [keep.tile([P, S], F32, name="a%d" % t) for t in range(PACK)]
         res = [keep.tile([P, S], F32, name="res%d" % t) for t in range(PACK)]
-        for t in range(PACK):
-            nc.gpsimd.memset(h[t][:, S:], 0.0)
 
-        def sigmoid(t):
-            nc.scalar.activation(sig[t][:], h_banks[t][:], ACT.Sigmoid, scale=SIXTEENTH)
+        def sigmoid(part):
+            bank, rows, stretch = part
+            nc.scalar.activation(sig[:, rows, stretch], bank[:], ACT.Sigmoid, scale=SIXTEENTH)
 
-        sigmoid(0)
-        for t in range(PACK):
-            nc.scalar.activation(h[t][:, :S], h_banks[t][:], ACT.Copy, scale=SIXTEENTH)
-            nc.scalar.activation(h_n2[t][:], h[t][:].indirect(n2_list[:]), ACT.Copy)
+        sigmoid(h_parts[0])
+        for bank, rows, stretch in h_parts:
+            nc.scalar.activation(h[:, rows, stretch], bank[:], ACT.Copy, scale=SIXTEENTH)
+        for t in (3, 0, 2, 1):
+            for u in range(2):
+                nc.scalar.activation(h_n2[t][:, cols(u)], h[:, t, :].indirect(half(n2_list, u)), ACT.Copy)
+        for part in h_parts[1:]:
+            sigmoid(part)
 
         def larger(t):
-            nc.vector.tensor_tensor(sm[t][:], h[t][:, :S], h_n2[t][:], ALU.max)
+            nc.vector.tensor_tensor(sm[t][:], h[:, t, :], h_n2[t][:], ALU.max)
 
-        k2_scales = coded_scales("k2", k2_list)
-        k2_words = coded_words("k2", k2_list)
-        two_scales = token_scales("two", two_list, False)
-        two_words = token_words("two", two_list, False)
-        b_banks = products("second", k2_words, k2_scales, two_words, two_scales)
-        larger(0)
-        larger(1)
-        cand_scales = token_scales("cand", cand_list, True)
-        cand_words = token_words("cand", cand_list, True)
-        larger(2)
-        larger(3)
+        k2_scales = coded_scales("k2", k2_list, "scales_in_turn")
+        k2_words = coded_words("k2", k2_list, "words_in_turn")
+        two_scales = token_scales("two", two_list, False, "scales_in_turn")
+        two_words = token_words("two", two_list, False, "words_in_turn")
+        b_banks = products("first", k2_words, k2_scales, two_words, two_scales)
+        for t in (3, 0, 2, 1):
+            larger(t)
 
-        for u in range(2):
-            for t in range(2):
-                nc.scalar.activation(ds[t][:].indirect(half(n1_list, u)), sm[t][:, cols(u)], ACT.Copy)
-            if u == 0:
-                for t in range(1, PACK):
-                    sigmoid(t)
-        for t in range(2, PACK):
-            nc.vector.tensor_copy(ds[t][:].indirect(n1_list[:]), sm[t][:])
+        def scatter_half(t, u):
+            nc.scalar.activation(ds[t][:].indirect(half(n1_list, u)), sm[t][:, cols(u)], ACT.Copy)
+
+        for t, u in ((0, 0), (0, 1), (1, 0), (1, 1)):
+            scatter_half(t, u)
+        nc.vector.tensor_copy(ds[3][:].indirect(n1_list[:]), sm[3][:])
+        nc.vector.tensor_copy(ds[2][:].indirect(n1_list[:]), sm[2][:])
+        cand_scales = token_scales("cand", cand_list, True, "sm3")
+        cand_words = token_words("cand", cand_list, True, "sm2")
 
         z_rows = keep.tile([P, PACK, S], BF16, name="z_rows", align_bytes=64)
-        for t in (2, 3, 0, 1):
-            nc.vector.scalar_tensor_tensor(
-                z_rows[:, t, :], ds[t][:, :S], gs_tile[:, t : t + 1], sig[t][:], ALU.mult, ALU.mult
-            )
+        gated = keep.tile([P, PACK, S], F32, name="gated")
+        for t in (3, 0, 2):
+            nc.gpsimd.tensor_scalar(gated[:, t, :], sig[:, t, :], gs_tile[:, t : t + 1], 0.0, ALU.mult, ALU.add)
+        for t in (3, 0, 2):
+            nc.gpsimd.tensor_tensor(z_rows[:, t, :], ds[t][:, :S], gated[:, t, :], ALU.mult)
+        nc.vector.scalar_tensor_tensor(z_rows[:, 1, :], ds[1][:], gs_tile[:, 1:2], sig[:, 1, :], ALU.mult, ALU.mult)
         z_woven = keep.tile([P, S, PACK], BF16, name="z_woven", align_bytes=64)
         nc.vector.tensor_copy(
             z_woven[:].rearrange("p (c i) t -> p c t i", i=4), z_rows[:].rearrange("p t (c i) -> p c t i", i=4)
@@ -189,19 +215,27 @@ def tile_picked_pqcjsoftbsendg_none_p_kernel(
             nc.scalar.activation(b[t][:], b_banks[t][:], ACT.Copy, scale=SIXTEENTH)
             nc.scalar.activation(tanh_b[t][:], b_banks[t][:], ACT.Tanh, scale=SIXTEENTH)
 
-        a_banks = products("first", cand_words, cand_scales, z_words, z_scales)
+        b_picked = keep.tile([P, S], F32, name="b_picked")
+        for u in range(2):
+            nc.scalar.activation(b_picked[:, cols(u)], b[3][:].indirect(half(n4_list, u)), ACT.Copy)
+
+        a_banks = products("second", cand_words, cand_scales, z_words, z_scales)
         for t in range(PACK):
             nc.scalar.activation(a[t][:], a_banks[t][:], ACT.Copy, scale=SIXTEENTH)
+        a_picked = keep.tile([P, 2, S], F32, name="a_picked")
+        for t in (2, 3):
+            for u in range(2):
+                nc.scalar.activation(a_picked[:, t - 2, cols(u)], a[t][:].indirect(half(n3_list, u)), ACT.Copy)
 
         out_rows = out.rearrange("(p t) c -> t p c", t=PACK)
-        for t in range(PACK):
+        for t in range(3):
             for u in range(2):
                 nc.vector.tensor_tensor(
                     tb[t][:, cols(u)], b[t][:].indirect(half(n4_list, u)), tanh_b[t][:, cols(u)], ALU.mult
                 )
+        nc.vector.tensor_tensor(tb[3][:], b_picked[:], tanh_b[3][:], ALU.mult)
         for t in range(PACK):
             for u in range(2):
-                nc.vector.tensor_tensor(
-                    res[t][:, cols(u)], a[t][:].indirect(half(n3_list, u)), tb[t][:, cols(u)], ALU.subtract
-                )
-            nc.sync.dma_start(out_rows[t], res[t][:])
+                looked_up = a_picked[:, t - 2, cols(u)] if t >= 2 else a[t][:].indirect(half(n3_list, u))
+                nc.vector.tensor_tensor(res[t][:, cols(u)], looked_up, tb[t][:, cols(u)], ALU.subtract)
+                nc.sync.dma_start(out_rows[t][:, cols(u)], res[t][:, cols(u)])

from contextlib import ExitStack

import concourse.mybir as mybir

K, T, S, G, H, C = 512, 1024, 512, 2048, 512, 512
FLOPS = 3 * 2 * 512 * 512 * 512

F32 = mybir.dt.float32
BF16 = mybir.dt.bfloat16
U32 = mybir.dt.uint32
I32 = mybir.dt.int32
U16 = mybir.dt.uint16
U8 = mybir.dt.uint8
FP8X4 = mybir.dt.float8_e4m3fn_x4
ACT = mybir.ActivationFunctionType
ALU = mybir.AluOpType

P = 128
PACK = 4
HALF = S // 2
SIXTEENTH = 0.0625
H_STRETCHES = ((0, 128), (128, 128), (256, 256))
DS_WIDE = 704


def tile_picked_pqcjsoftbsendg_none_p_kernel(
    tc, x_words, x_scales, d_words, d_scales, gs, offs, k1, n1, n2, cand, two, k2, n3, n4, out
):
    nc = tc.nc
    with ExitStack() as ctx:
        lists = ctx.enter_context(tc.tile_pool(name="lists", bufs=1))
        keep = ctx.enter_context(tc.tile_pool(name="keep", bufs=1))
        psum = ctx.enter_context(tc.psum_pool(name="psum", bufs=1))

        def load_list(name, dram):
            tile = lists.tile([P, S // 16], U16, name=name)
            nc.sync.dma_start(tile[:], dram)
            return tile

        def half(offsets, u):
            return offsets[:, 16 * u : 16 * (u + 1)]

        def cols(u):
            return slice(HALF * u, HALF * (u + 1))

        d_scale_win = keep.tile([P, G], U8, name="d_scale_win", align_bytes=64)
        x_scale_win = keep.tile([P, T], U8, name="x_scale_win", align_bytes=64)
        nc.vector.memset(d_scale_win[:].bitcast(I32), 0)
        nc.gpsimd.memset(x_scale_win[:].bitcast(I32), 0)
        k1_list = load_list("k1_list", k1)
        nc.sync.dma_start(d_scale_win[0:P:8, :].bitcast(I32), d_scales[0].bitcast(I32))
        offs_list = load_list("offs_list", offs)
        x_win = keep.tile([P, T], I32, name="x_win", align_bytes=64)
        d_win = keep.tile([P, G], I32, name="d_win", align_bytes=64)
        for r in range(PACK):
            nc.sync.dma_start(x_scale_win[r:P:32, :].bitcast(I32), x_scales[0, r:16:PACK, :].bitcast(I32))
        nc.sync.dma_start(d_win[:], d_words[0].rearrange("p n t -> p (n t)").bitcast(I32))
        nc.sync.dma_start(x_win[:], x_words[0].rearrange("p n t -> p (n t)").bitcast(I32))
        gs_tile = keep.tile([P, PACK], F32, name="gs_tile")

        def coded_scales(name, offsets, tag):
            plane = keep.tile([P, H], U8, name=name + "_plane", align_bytes=64)
            nc.vector.memset(plane[:].bitcast(I32), 0)
            picked = keep.tile([P, H], U8, name=name + "_picked_scales", tag=tag, align_bytes=64)
            nc.vector.tensor_copy(picked[:], d_scale_win[:].indirect(offsets[:]))
            dealt = keep.tile([P, H], U8, name=name + "_dealt_scales", align_bytes=64)
            nc.vector.tensor_copy(
                dealt[:].rearrange("p (t m) -> p m t", t=PACK), picked[:].rearrange("p (m t) -> p m t", t=PACK)
            )
            for r in range(PACK):
                nc.sync.dma_start(plane[r:P:32, :].bitcast(I32), dealt[8 * r : P : 32, :].bitcast(I32))
            return plane

        def coded_words(name, offsets, tag):
            picked = keep.tile([P, H], U32, name=name + "_picked_words", tag=tag, align_bytes=64)
            nc.vector.tensor_copy(picked[:], d_win[:].bitcast(U32).indirect(offsets[:]))
            dealt = keep.tile([P, H], U32, name=name + "_dealt_words", align_bytes=64)
            nc.vector.tensor_copy(
                dealt[:].rearrange("p (t m) -> p m t", t=PACK), picked[:].rearrange("p (m t) -> p m t", t=PACK)
            )
            return dealt

        def token_scales(name, offsets, deal, tag):
            picked = keep.tile([P, S], U8, name=name + "_scales", tag=tag, align_bytes=64)
            view = picked[:].rearrange("p (t m) -> p m t", t=PACK) if deal else picked[:]
            nc.vector.tensor_copy(view, x_scale_win[:].indirect(offsets[:]))
            return picked

        def token_words(name, offsets, deal, tag):
            picked = keep.tile([P, S], U32, name=name + "_words", tag=tag, align_bytes=64)
            view = picked[:].rearrange("p (t m) -> p m t", t=PACK) if deal else picked[:]
            nc.vector.tensor_copy(view, x_win[:].bitcast(U32).indirect(offsets[:]))
            return picked

        def products(tag, lhs_words, lhs_scales, rhs_words, rhs_scales):
            banks = []
            for t in range(PACK):
                bank = psum.tile([P, S], F32, name=tag + str(t))
                m = slice(P * t, P * (t + 1))
                nc.tensor.matmul_mx(
                    out=bank[:],
                    lhsT=lhs_words[:, m].bitcast(FP8X4),
                    lhsT_scale=lhs_scales[:, m],
                    rhs=rhs_words[:].bitcast(FP8X4),
                    rhs_scale=rhs_scales[:],
                    start=True,
                    stop=True,
                )
                banks.append(bank)
            return banks

        k1_scales = coded_scales("k1", k1_list, "k1_scales")
        lead = H_STRETCHES[0][1]
        lead_scales = keep.tile([P, lead], U8, name="lead_scales", tag="scales_in_turn", align_bytes=64)
        rest_scales = keep.tile([P, S - lead], U8, name="rest_scales", align_bytes=64)
        nc.vector.tensor_copy(lead_scales[:], x_scale_win[:].indirect(offs_list[:, : lead // 16]))
        nc.vector.tensor_copy(rest_scales[:], x_scale_win[:].indirect(offs_list[:, lead // 16 :]))
        k1_words = coded_words("k1", k1_list, "k1_words")
        h_parts = []
        for first, width in H_STRETCHES:
            stretch = slice(first, first + width)
            entries = offs_list[:, first // 16 : (first + width) // 16]
            offs_scales = lead_scales[:] if first == 0 else rest_scales[:, first - lead : first - lead + width]
            words_tag = "words_in_turn" if first == 0 else "offs_words%d" % first
            offs_words = keep.tile([P, width], U32, name="offs_words", tag=words_tag, align_bytes=64)
            nc.vector.tensor_copy(offs_words[:], x_win[:].bitcast(U32).indirect(entries))
            per_bank = S // width
            for t0 in range(0, PACK, per_bank):
                bank = psum.tile([P, per_bank, width], F32, name="first%d" % len(h_parts))
                for t in range(t0, t0 + per_bank):
                    m = slice(P * t, P * (t + 1))
                    nc.tensor.matmul_mx(
                        out=bank[:, t - t0, :],
                        lhsT=k1_words[:, m].bitcast(FP8X4),
                        lhsT_scale=k1_scales[:, m],
                        rhs=offs_words[:].bitcast(FP8X4),
                        rhs_scale=offs_scales,
                        start=True,
                        stop=True,
                    )
                h_parts.append((bank, slice(t0, t0 + per_bank), stretch))

        k2_list = load_list("k2_list", k2)
        two_list = load_list("two_list", two)
        n2_list = load_list("n2_list", n2)
        cand_list = load_list("cand_list", cand)
        n1_list = load_list("n1_list", n1)
        n4_list = load_list("n4_list", n4)
        n3_list = load_list("n3_list", n3)
        nc.sync.dma_start(gs_tile[:], gs.rearrange("(p t) o -> p (t o)", t=PACK))

        h = keep.tile([P, PACK, S], F32, name="h", align_bytes=64)
        h_n2 = [keep.tile([P, S], F32, name="h_n2_%d" % t) for t in range(PACK)]
        sig = keep.tile([P, PACK, S], F32, name="sig")
        sm = [keep.tile([P, S], F32, name="sm%d" % t, align_bytes=64) for t in range(PACK)]
        ds = [keep.tile([P, S if t < 2 else DS_WIDE], F32, name="ds%d" % t) for t in range(PACK)]
        b = [keep.tile([P, S], F32, name="b%d" % t) for t in range(PACK)]
        tanh_b = [keep.tile([P, S], F32, name="tanh_b%d" % t) for t in range(PACK)]
        tb = [keep.tile([P, S], F32, name="tb%d" % t) for t in range(PACK)]
        a = [keep.tile([P, S], F32, name="a%d" % t) for t in range(PACK)]
        res = [keep.tile([P, S], F32, name="res%d" % t) for t in range(PACK)]

        def sigmoid(part):
            bank, rows, stretch = part
            nc.scalar.activation(sig[:, rows, stretch], bank[:], ACT.Sigmoid, scale=SIXTEENTH)

        sigmoid(h_parts[0])
        for bank, rows, stretch in h_parts:
            nc.scalar.activation(h[:, rows, stretch], bank[:], ACT.Copy, scale=SIXTEENTH)
        for t in (3, 0, 2, 1):
            for u in range(2):
                nc.scalar.activation(h_n2[t][:, cols(u)], h[:, t, :].indirect(half(n2_list, u)), ACT.Copy)
        for part in h_parts[1:]:
            sigmoid(part)

        def larger(t):
            nc.vector.tensor_tensor(sm[t][:], h[:, t, :], h_n2[t][:], ALU.max)

        k2_scales = coded_scales("k2", k2_list, "scales_in_turn")
        k2_words = coded_words("k2", k2_list, "words_in_turn")
        two_scales = token_scales("two", two_list, False, "scales_in_turn")
        two_words = token_words("two", two_list, False, "words_in_turn")
        b_banks = products("first", k2_words, k2_scales, two_words, two_scales)
        for t in (3, 0, 2, 1):
            larger(t)

        def scatter_half(t, u):
            nc.scalar.activation(ds[t][:].indirect(half(n1_list, u)), sm[t][:, cols(u)], ACT.Copy)

        for t, u in ((0, 0), (0, 1), (1, 0), (1, 1)):
            scatter_half(t, u)
        nc.vector.tensor_copy(ds[3][:].indirect(n1_list[:]), sm[3][:])
        nc.vector.tensor_copy(ds[2][:].indirect(n1_list[:]), sm[2][:])
        cand_scales = token_scales("cand", cand_list, True, "sm3")
        cand_words = token_words("cand", cand_list, True, "sm2")

        z_rows = keep.tile([P, PACK, S], BF16, name="z_rows", align_bytes=64)
        gated = keep.tile([P, PACK, S], F32, name="gated")
        for t in (3, 0, 2):
            nc.gpsimd.tensor_scalar(gated[:, t, :], sig[:, t, :], gs_tile[:, t : t + 1], 0.0, ALU.mult, ALU.add)
        for t in (3, 0, 2):
            nc.gpsimd.tensor_tensor(z_rows[:, t, :], ds[t][:, :S], gated[:, t, :], ALU.mult)
        nc.vector.scalar_tensor_tensor(z_rows[:, 1, :], ds[1][:], gs_tile[:, 1:2], sig[:, 1, :], ALU.mult, ALU.mult)
        z_woven = keep.tile([P, S, PACK], BF16, name="z_woven", align_bytes=64)
        nc.vector.tensor_copy(
            z_woven[:].rearrange("p (c i) t -> p c t i", i=4), z_rows[:].rearrange("p t (c i) -> p c t i", i=4)
        )
        z_words = keep.tile([P, S], U32, name="z_words", align_bytes=64)
        z_scales = keep.tile([P, S], U8, name="z_scales", align_bytes=64)
        nc.vector.quantize_mx(
            out=z_words[:].bitcast(FP8X4), scales=z_scales[:], in_=z_woven[:].rearrange("p c t -> p (c t)")
        )

        for t in range(PACK):
            nc.scalar.activation(b[t][:], b_banks[t][:], ACT.Copy, scale=SIXTEENTH)
            nc.scalar.activation(tanh_b[t][:], b_banks[t][:], ACT.Tanh, scale=SIXTEENTH)

        b_picked = keep.tile([P, S], F32, name="b_picked")
        for u in range(2):
            nc.scalar.activation(b_picked[:, cols(u)], b[3][:].indirect(half(n4_list, u)), ACT.Copy)

        a_banks = products("second", cand_words, cand_scales, z_words, z_scales)
        for t in range(PACK):
            nc.scalar.activation(a[t][:], a_banks[t][:], ACT.Copy, scale=SIXTEENTH)
        a_picked = keep.tile([P, 2, S], F32, name="a_picked")
        for t in (2, 3):
            for u in range(2):
                nc.scalar.activation(a_picked[:, t - 2, cols(u)], a[t][:].indirect(half(n3_list, u)), ACT.Copy)

        out_rows = out.rearrange("(p t) c -> t p c", t=PACK)
        for t in range(3):
            for u in range(2):
                nc.vector.tensor_tensor(
                    tb[t][:, cols(u)], b[t][:].indirect(half(n4_list, u)), tanh_b[t][:, cols(u)], ALU.mult
                )
        nc.vector.tensor_tensor(tb[3][:], b_picked[:], tanh_b[3][:], ALU.mult)
        for t in range(PACK):
            for u in range(2):
                looked_up = a_picked[:, t - 2, cols(u)] if t >= 2 else a[t][:].indirect(half(n3_list, u))
                nc.vector.tensor_tensor(res[t][:, cols(u)], looked_up, tb[t][:, cols(u)], ALU.subtract)
                nc.sync.dma_start(out_rows[t][:, cols(u)], res[t][:, cols(u)])
